import numpy as np
import ml_dtypes


def mxq(x, axis, fmt="e4m3"):
    dtype, down = {"e4m3": (ml_dtypes.float8_e4m3fn, 7), "e5m2": (ml_dtypes.float8_e5m2, 14)}[fmt]
    v = np.moveaxis(np.asarray(x, np.float32).astype(ml_dtypes.bfloat16).astype(np.float64), axis, -1)
    blocks = v.reshape(v.shape[:-1] + (-1, 32))
    amax = np.abs(blocks).max(-1, keepdims=True)
    byte = np.maximum(np.where(amax > 0, np.frexp(amax)[1] - 1 + 127, 0) - down, 1)
    scale = np.exp2(byte - 127.0)
    codes = (blocks / scale).astype(np.float32).astype(dtype).astype(np.float64)
    return np.moveaxis((codes * scale).reshape(v.shape), -1, axis)


WIDE = False


def mx_kscale(k):
    if not WIDE:
        return np.ones(k)
    levels = np.array([10, -10, 5, -5, 0])
    if k % 512:
        return np.exp2(np.random.permutation(np.resize(levels, k // 32))).repeat(32)
    a = np.empty((k // 512, 16))
    for p in range(k // 512):
        a[p, :8] = np.random.permutation(np.resize(levels, 8))
        for g in range(8):
            far = levels[np.abs(levels - a[p, g]) >= 10]
            a[p, g + 8] = far[np.random.randint(len(far))]
    return np.exp2(a.ravel()).repeat(32)


def f64(x):
    return np.asarray(x).astype(np.float64)


def striped(idx):
    return np.tile(idx.reshape(-1, 16).T, (8, 1)).astype(np.uint16)


def unstriped(offs):
    return offs[:16].T.reshape(-1).astype(np.int64)


def pack_weight(w):
    k, n = w.shape
    w = f64(np.asarray(w, np.float32).astype(ml_dtypes.bfloat16)).reshape(k // 32, 32, n)
    amax = np.abs(w).max(1)
    byte = np.clip(np.where(amax > 0, np.frexp(amax)[1] - 1 + 127 - 7, 1), 1, 254)
    scaled = (w * np.exp2(127.0 - byte)[:, None, :]).reshape(k, n).astype(np.float32)
    words = np.ascontiguousarray(scaled.reshape(k // 512, 128, 4, n).transpose(0, 1, 3, 2)).astype(ml_dtypes.float8_e4m3fn).view(np.uint8)
    return words, np.ascontiguousarray(byte.astype(np.uint8).reshape(k // 512, 16, n))


def unpack_weight(words, scales):
    g, p, n, _ = words.shape
    vals = np.ascontiguousarray(words).view(ml_dtypes.float8_e4m3fn).astype(np.float64) * np.repeat(np.exp2(scales.astype(np.float64) - 127.0), 8, axis=1)[..., None]
    return vals.transpose(0, 1, 3, 2).reshape(g * 512, n)


def sigmoid(v):
    return 1.0 / (1.0 + np.exp(-np.maximum(v, -700.0)))


K, T, S, N, H, W = 512, 2048, 512, 512, 512, 2048


def setup_inputs():
    n = np.random.standard_normal
    s = mx_kscale(K)[:, None]
    u = mx_kscale(H)
    packed_xT = pack_weight(n((K, T)) * s)
    return {
        "x_words": packed_xT[0],
        "x_scales": packed_xT[1],
        "w1": (n((K, H)) / np.sqrt(K) / s).astype(np.float32),
        "gn": (np.random.uniform(0.5, 1.5, (H, 1)) * u[:, None]).astype(np.float32),
        "w2": (n((H, N)) / np.sqrt(2 * H) / u[:, None]).astype(np.float32),
        "w3": (n((K, N)) / np.sqrt(2 * K) / s).astype(np.float32),
        "offs": striped(np.random.permutation(T)[:S]),
        "n1": striped(np.random.randint(0, S, W)),
        "two": striped(np.random.permutation(T)[:S]),
        "n2": striped(np.random.permutation(S)),
        "n3": striped(np.random.permutation(S)),
        "n4": striped(np.random.permutation(S)),
    }


def reference(x_words, x_scales, w1, gn, w2, w3, offs, n1, two, n2, n3, n4):
    xq = unpack_weight(x_words, x_scales)[:, unstriped(offs)]
    y = mxq(f64(w1), 0, "e4m3").T @ xq
    mb = y[:, unstriped(n1)]
    ms = mb.reshape(H, S, 4).sum(axis=2)
    z = f64(gn) * (y * sigmoid(ms))
    x_two = unpack_weight(x_words, x_scales)[:, unstriped(two)]
    h = mxq(f64(w2), 0, "e4m3").T @ mxq(z, 0, "e4m3") + mxq(f64(w3), 0, "e4m3").T @ x_two
    st = h - h[:, unstriped(n2)]
    su = np.maximum(st, st[:, unstriped(n3)])
    return su + 0.5 * su[:, unstriped(n4)]

@@ -1,0 +1,224 @@
+from contextlib import ExitStack
+
+import concourse.mybir as mybir
+
+K, T, S, N, H = 512, 2048, 512, 512, 512
+FLOPS = 2 * S * (K * H + H * N + K * N)
+
+F32 = mybir.dt.float32
+BF16 = mybir.dt.bfloat16
+I32 = mybir.dt.int32
+U32 = mybir.dt.uint32
+U16 = mybir.dt.uint16
+U8 = mybir.dt.uint8
+FP8X4 = mybir.dt.float8_e4m3fn_x4
+ALU = mybir.AluOpType
+ACT = mybir.ActivationFunctionType
+
+P = 128
+PACK = 4
+MEMBERS = 4
+WINDOW = S + 16
+CHUNK = 128
+CHUNKS = S // CHUNK
+SCALAR_COLS = 24
+
+
+def tile_picked_mixingsumgthree_none_p_kernel(
+    tc, x_words, x_scales, w1, gn, w2, w3, offs, n1, two, n2, n3, n4, out
+):
+    nc = tc.nc
+    with ExitStack() as ctx:
+        keep = ctx.enter_context(tc.tile_pool(name="keep", bufs=1))
+        psum = ctx.enter_context(tc.psum_pool(name="psum", bufs=1))
+
+        def load_list(src, name):
+            tile = keep.tile(list(src.shape), U16, name=name)
+            nc.sync.dma_start(tile[:], src)
+            return tile
+
+        def load_weight(src, name):
+            tile = keep.tile([P, PACK, src.shape[1]], F32, name=name, tag="weight_raw")
+            nc.sync.dma_start(out=tile[:], in_=src.rearrange("(p j) c -> p j c", j=PACK))
+            return tile
+
+        def gather(on_vector, dst, window, offsets):
+            if on_vector:
+                nc.vector.tensor_copy(dst, window.indirect(offsets))
+            else:
+                nc.scalar.activation(dst, window.indirect(offsets), ACT.Copy)
+
+        def mx_tiles(name, width, tag=""):
+            codes = keep.tile([P, width], U32, name=name + "_codes", tag=tag, align_bytes=64)
+            scales = keep.tile([P, width], U8, name=name + "_scales", align_bytes=64)
+            return codes, scales
+
+        def quantize(mx, cols, src):
+            nc.vector.quantize_mx(out=mx[0][:, cols].bitcast(FP8X4), scales=mx[1][:, cols], in_=src)
+
+        def product(dst, lhs, lhs_cols, rhs, rhs_cols, start, stop):
+            nc.tensor.matmul_mx(
+                out=dst,
+                lhsT=lhs[0][:, lhs_cols].bitcast(FP8X4),
+                lhsT_scale=lhs[1][:, lhs_cols],
+                rhs=rhs[0][:, rhs_cols].bitcast(FP8X4),
+                rhs_scale=rhs[1][:, rhs_cols],
+                start=start,
+                stop=stop,
+            )
+
+        def interleave_views(grouped, raw):
+            return (
+                grouped.rearrange("p (c i j) -> p c j i", i=4, j=PACK),
+                raw.rearrange("p j (c i) -> p c j i", i=4),
+            )
+
+        table_scales = keep.tile([P, T], U8, name="table_scales")
+        nc.vector.memset(table_scales[:].bitcast(I32), 0)
+        offs_sb = load_list(offs, "offs_sb")
+        two_sb = load_list(two, "two_sb")
+        w1_raw = load_weight(w1, "w1_raw")
+        for r in range(4):
+            nc.scalar.dma_start(
+                out=table_scales[r:P:32, :].bitcast(I32), in_=x_scales[0, r:16:4, :].bitcast(I32)
+            )
+        table_words = keep.tile([P, T], U32, name="table_words")
+        nc.sync.dma_start(
+            out=table_words[:].bitcast(I32),
+            in_=x_words[0].rearrange("p c r -> p (c r)").bitcast(I32),
+        )
+        n1_sb = load_list(n1, "n1_sb")
+        gain = keep.tile([P, PACK], F32, name="gain")
+        nc.sync.dma_start(out=gain[:], in_=gn.rearrange("(p t) o -> p (t o)", t=PACK))
+        n2_sb = load_list(n2, "n2_sb")
+        n3_sb = load_list(n3, "n3_sb")
+        n4_sb = load_list(n4, "n4_sb")
+
+        w1_mx = [mx_tiles(f"w1_{a}", 2 * P) for a in range(2)]
+        w1_bf = [
+            keep.tile([P, 2 * P * PACK], BF16, name=f"w1_bf{a}", tag=f"w1_bf{a}", align_bytes=64) for a in range(2)
+        ]
+        w1_view = w1_raw[:].rearrange("p j (m t) -> p m j t", t=PACK)
+        for a in range(2):
+            nc.scalar.copy(
+                out=w1_bf[a][:].rearrange("p (t m j) -> p m j t", t=2, j=PACK),
+                in_=w1_view[:, :, :, 2 * a : 2 * a + 2],
+            )
+        w2_raw = load_weight(w2, "w2_raw")
+        x_one = mx_tiles("x_one", S)
+        x_two = mx_tiles("x_two", S)
+        nc.vector.tensor_copy(x_one[1][:], table_scales[:].indirect(offs_sb[:]))
+        nc.vector.tensor_copy(x_two[1][:], table_scales[:].indirect(two_sb[:]))
+        quantize(w1_mx[0], slice(0, 2 * P), w1_bf[0][:])
+        nc.vector.tensor_copy(x_one[0][:], table_words[:].indirect(offs_sb[:]))
+        quantize(w1_mx[1], slice(0, 2 * P), w1_bf[1][:])
+        nc.vector.tensor_copy(x_two[0][:], table_words[:].indirect(two_sb[:]))
+
+        y = []
+        y_gain = keep.tile([P, PACK, S], F32, name="y_gain")
+        for t in range(PACK):
+            bank = psum.tile([P, S], F32, name=f"y_bank{t}")
+            product(bank[:], w1_mx[t // 2], slice(P * (t % 2), P * (t % 2 + 1)), x_one, slice(0, S), True, True)
+            y_t = keep.tile([P, WINDOW], F32, name=f"y{t}")
+            copy = nc.vector.tensor_copy if t % 2 else nc.scalar.copy
+            copy(out=y_t[:, :S], in_=bank[:])
+            y.append(y_t)
+
+        w2_mx = mx_tiles("w2", N)
+        w3_mx = [mx_tiles(f"w3_{a}", N // 2) for a in range(2)]
+        z_mx = mx_tiles("z", S)
+        h_bank = [psum.tile([P, S], F32, name=f"h_bank{m}") for m in range(N // P)]
+        members = [keep.tile([P, PACK, MEMBERS * CHUNK], F32, name=f"members{b}", align_bytes=64) for b in range(2)]
+        pairs = keep.tile([P, CHUNK, PACK, 2], F32, name="pairs")
+        gates = [keep.tile([P, CHUNK * PACK], F32, name=f"gates{b}") for b in range(2)]
+        z_bf = [keep.tile([P, CHUNK * PACK], BF16, name=f"z_bf{b}", align_bytes=64) for b in range(2)]
+
+        def fetch_members(u, t):
+            cols = MEMBERS * CHUNK // 16
+            gather(t == 3, members[u % 2][:, t, :], y[t][:], n1_sb[:, u * cols : (u + 1) * cols])
+
+        def add_pairs(u, a):
+            view = members[u % 2][:].rearrange("p t (j s e) -> p j t s e", s=2, e=2)
+            planes = slice(2 * a, 2 * a + 2)
+            nc.vector.tensor_tensor(pairs[:, :, planes, :], view[:, :, planes, 0, :], view[:, :, planes, 1, :], ALU.add)
+
+        def gate(u):
+            sums = members[u % 2][:, :, :CHUNK]
+            view = pairs[:].rearrange("p (q j) t e -> p q (j t) e", q=PACK)
+            nc.vector.tensor_tensor(sums, view[:, :, :, 0], view[:, :, :, 1], ALU.add)
+            nc.scalar.activation(gates[u % 2][:].rearrange("p (q c) -> p q c", q=PACK), sums, ACT.Sigmoid)
+
+        def hidden(u):
+            cols = slice(u * CHUNK, (u + 1) * CHUNK)
+            nc.vector.tensor_tensor(
+                z_bf[u % 2][:].rearrange("p (j t) -> p j t", t=PACK),
+                gates[u % 2][:].rearrange("p (j t) -> p j t", t=PACK),
+                y_gain[:, :, cols].rearrange("p t j -> p j t"),
+                ALU.mult,
+            )
+            quantize(z_mx, cols, z_bf[u % 2][:])
+
+        def second_layer(u):
+            cols = slice(u * CHUNK, (u + 1) * CHUNK)
+            for m in range(N // P):
+                product(h_bank[m][:, cols], w2_mx, slice(m * P, (m + 1) * P), z_mx, cols, u == 0, u == CHUNKS - 1)
+
+        def side_weights(a):
+            w3_bf = members[a][:, 0, :].bitcast(BF16)
+            dst, src = interleave_views(w3_bf, w3_raw[:, :, a * N // 2 : (a + 1) * N // 2])
+            nc.scalar.copy(out=dst, in_=src)
+            quantize(w3_mx[a], slice(0, N // 2), w3_bf)
+
+        for u in range(CHUNKS):
+            for t in range(PACK):
+                fetch_members(u, t)
+            if u == 0:
+                for t in range(PACK):
+                    nc.vector.tensor_scalar(y_gain[:, t, :], y[t][:, :S], gain[:, t : t + 1], None, ALU.mult)
+            if u == 1:
+                w2_bf = keep.tile([P, N * PACK], BF16, name="w2_bf", align_bytes=64)
+                dst, src = interleave_views(w2_bf[:], w2_raw[:])
+                nc.vector.tensor_copy(out=dst, in_=src)
+                w3_raw = load_weight(w3, "w3_raw")
+                quantize(w2_mx, slice(0, N), w2_bf[:])
+            if u > 0:
+                hidden(u - 1)
+                second_layer(u - 1)
+            add_pairs(u, 0)
+            add_pairs(u, 1)
+            gate(u)
+
+        last = slice(S - CHUNK, S)
+        side_weights(0)
+        hidden(CHUNKS - 1)
+        side_weights(1)
+        for m in range(N // P):
+            for cols in (slice(0, 256), slice(256, 384), last):
+                product(h_bank[m][:, cols], w3_mx[m // 2], slice((m % 2) * P, (m % 2 + 1) * P), x_two, cols, False, False)
+            product(h_bank[m][:, last], w2_mx, slice(m * P, (m + 1) * P), z_mx, last, False, True)
+
+        tiles = range(N // P)
+        h = [keep.tile([P, S], F32, name=f"h{m}") for m in tiles]
+        st = [keep.tile([P, S], F32, name=f"st{m}") for m in tiles]
+        su = [keep.tile([P, S], F32, name=f"su{m}") for m in tiles]
+        picked = [keep.tile([P, S], F32, name=f"picked{m}") for m in tiles]
+        result = [keep.tile([P, S], F32, name=f"result{m}") for m in tiles]
+
+        def gather_split(m, window, offsets):
+            cut = 16 * SCALAR_COLS
+            gather(False, picked[m][:, :cut], window[:], offsets[:, :SCALAR_COLS])
+            gather(True, picked[m][:, cut:], window[:], offsets[:, SCALAR_COLS:])
+
+        for m in tiles:
+            copy = nc.vector.tensor_copy if m % 2 else nc.scalar.copy
+            copy(out=h[m][:], in_=h_bank[m][:])
+        for m in tiles:
+            gather_split(m, h[m], n2_sb)
+            nc.vector.tensor_tensor(st[m][:], h_bank[m][:], picked[m][:], ALU.subtract)
+        for m in tiles:
+            gather_split(m, st[m], n3_sb)
+            nc.vector.tensor_tensor(su[m][:], st[m][:], picked[m][:], ALU.max)
+        for m in tiles:
+            gather_split(m, su[m], n4_sb)
+            nc.vector.scalar_tensor_tensor(result[m][:], picked[m][:], 0.5, su[m][:], ALU.mult, ALU.add)
+            nc.sync.dma_start(out=out[m * P : (m + 1) * P, :], in_=result[m][:])

@@ -1,6 +1,7 @@
 from contextlib import ExitStack
 
 import concourse.mybir as mybir
+from concourse.masks import make_identity
 
 K, T, S, N, H = 512, 2048, 512, 512, 512
 FLOPS = 2 * S * (K * H + H * N + K * N)
@@ -22,6 +23,8 @@ WINDOW = S + 16
 CHUNK = 128
 CHUNKS = S // CHUNK
 SCALAR_COLS = 24
+TURNED = 2
+VECTOR_PLANES = (2, 2, 1, 1)
 
 
 def tile_picked_mixingsumgthree_none_p_kernel(
@@ -74,14 +77,14 @@ def tile_picked_mixingsumgthree_none_p_kernel(
             )
 
         table_scales = keep.tile([P, T], U8, name="table_scales")
-        nc.vector.memset(table_scales[:].bitcast(I32), 0)
+        nc.gpsimd.memset(table_scales[:].bitcast(I32), 0)
         offs_sb = load_list(offs, "offs_sb")
         two_sb = load_list(two, "two_sb")
-        w1_raw = load_weight(w1, "w1_raw")
         for r in range(4):
-            nc.scalar.dma_start(
+            nc.sync.dma_start(
                 out=table_scales[r:P:32, :].bitcast(I32), in_=x_scales[0, r:16:4, :].bitcast(I32)
             )
+        w1_raw = load_weight(w1, "w1_raw")
         table_words = keep.tile([P, T], U32, name="table_words")
         nc.sync.dma_start(
             out=table_words[:].bitcast(I32),
@@ -94,13 +97,17 @@ def tile_picked_mixingsumgthree_none_p_kernel(
         n3_sb = load_list(n3, "n3_sb")
         n4_sb = load_list(n4, "n4_sb")
 
+        identity = keep.tile([P, P], F32, name="identity")
+        make_identity(nc, identity[:])
+
         w1_mx = [mx_tiles(f"w1_{a}", 2 * P) for a in range(2)]
         w1_bf = [
             keep.tile([P, 2 * P * PACK], BF16, name=f"w1_bf{a}", tag=f"w1_bf{a}", align_bytes=64) for a in range(2)
         ]
         w1_view = w1_raw[:].rearrange("p j (m t) -> p m j t", t=PACK)
         for a in range(2):
-            nc.scalar.copy(
+            copy = nc.vector.tensor_copy if a == 0 else nc.scalar.copy
+            copy(
                 out=w1_bf[a][:].rearrange("p (t m j) -> p m j t", t=2, j=PACK),
                 in_=w1_view[:, :, :, 2 * a : 2 * a + 2],
             )
@@ -110,17 +117,17 @@ def tile_picked_mixingsumgthree_none_p_kernel(
         nc.vector.tensor_copy(x_one[1][:], table_scales[:].indirect(offs_sb[:]))
         nc.vector.tensor_copy(x_two[1][:], table_scales[:].indirect(two_sb[:]))
         quantize(w1_mx[0], slice(0, 2 * P), w1_bf[0][:])
-        nc.vector.tensor_copy(x_one[0][:], table_words[:].indirect(offs_sb[:]))
         quantize(w1_mx[1], slice(0, 2 * P), w1_bf[1][:])
+        nc.vector.tensor_copy(x_one[0][:], table_words[:].indirect(offs_sb[:]))
         nc.vector.tensor_copy(x_two[0][:], table_words[:].indirect(two_sb[:]))
 
         y = []
         y_gain = keep.tile([P, PACK, S], F32, name="y_gain")
         for t in range(PACK):
-            bank = psum.tile([P, S], F32, name=f"y_bank{t}")
+            bank = psum.tile([P, S], F32, name=f"y_bank{t}", tag=f"bank{t}")
             product(bank[:], w1_mx[t // 2], slice(P * (t % 2), P * (t % 2 + 1)), x_one, slice(0, S), True, True)
             y_t = keep.tile([P, WINDOW], F32, name=f"y{t}")
-            copy = nc.vector.tensor_copy if t % 2 else nc.scalar.copy
+            copy = nc.vector.tensor_copy if t > 0 else nc.scalar.copy
             copy(out=y_t[:, :S], in_=bank[:])
             y.append(y_t)
 
@@ -128,31 +135,61 @@ def tile_picked_mixingsumgthree_none_p_kernel(
         w3_mx = [mx_tiles(f"w3_{a}", N // 2) for a in range(2)]
         z_mx = mx_tiles("z", S)
         h_bank = [psum.tile([P, S], F32, name=f"h_bank{m}") for m in range(N // P)]
-        members = [keep.tile([P, PACK, MEMBERS * CHUNK], F32, name=f"members{b}", align_bytes=64) for b in range(2)]
+        members = [keep.tile([P, PACK, MEMBERS * CHUNK], F32, name=f"members{u}") for u in range(CHUNKS)]
         pairs = keep.tile([P, CHUNK, PACK, 2], F32, name="pairs")
-        gates = [keep.tile([P, CHUNK * PACK], F32, name=f"gates{b}") for b in range(2)]
+        sums = {}
+        gates = {}
         z_bf = [keep.tile([P, CHUNK * PACK], BF16, name=f"z_bf{b}", align_bytes=64) for b in range(2)]
 
-        def fetch_members(u, t):
+        def fetch_members(u):
             cols = MEMBERS * CHUNK // 16
-            gather(t == 3, members[u % 2][:, t, :], y[t][:], n1_sb[:, u * cols : (u + 1) * cols])
+            for t in range(PACK):
+                on_vector = t >= PACK - VECTOR_PLANES[u]
+                gather(on_vector, members[u][:, t, :], y[t][:], n1_sb[:, u * cols : (u + 1) * cols])
 
-        def add_pairs(u, a):
-            view = members[u % 2][:].rearrange("p t (j s e) -> p j t s e", s=2, e=2)
-            planes = slice(2 * a, 2 * a + 2)
-            nc.vector.tensor_tensor(pairs[:, :, planes, :], view[:, :, planes, 0, :], view[:, :, planes, 1, :], ALU.add)
+        def add_members(u):
+            if u < TURNED:
+                sums[u] = psum.tile([P, PACK * P], F32, name=f"sums{u}", tag=f"bank{u % 2}")
+                for t in range(PACK):
+                    for s in range(MEMBERS):
+                        nc.tensor.matmul(
+                            sums[u][:, t * P : (t + 1) * P],
+                            members[u][:, t, s::MEMBERS],
+                            identity[:],
+                            start=s == 0,
+                            stop=s == MEMBERS - 1,
+                            is_transpose=True,
+                        )
+            else:
+                view = members[u][:].rearrange("p t (j s e) -> p j t s e", s=2, e=2)
+                for a in range(2):
+                    planes = slice(2 * a, 2 * a + 2)
+                    nc.vector.tensor_tensor(
+                        pairs[:, :, planes, :], view[:, :, planes, 0, :], view[:, :, planes, 1, :], ALU.add
+                    )
+                sums[u] = keep.tile([P, CHUNK * PACK], F32, name=f"sums{u}", align_bytes=64)
+                view = pairs[:].rearrange("p j t e -> p (j t) e")
+                nc.vector.tensor_tensor(sums[u][:], view[:, :, 0], view[:, :, 1], ALU.add)
 
         def gate(u):
-            sums = members[u % 2][:, :, :CHUNK]
-            view = pairs[:].rearrange("p (q j) t e -> p q (j t) e", q=PACK)
-            nc.vector.tensor_tensor(sums, view[:, :, :, 0], view[:, :, :, 1], ALU.add)
-            nc.scalar.activation(gates[u % 2][:].rearrange("p (q c) -> p q c", q=PACK), sums, ACT.Sigmoid)
+            gates[u] = keep.tile([P, CHUNK * PACK], F32, name=f"gates{u}", align_bytes=64)
+            nc.scalar.activation(gates[u][:], sums[u][:], ACT.Sigmoid)
+
+        def turn_back(u):
+            turned = gates[u]
+            gates[u] = psum.tile([P, PACK, CHUNK], F32, name=f"back{u}", tag=f"bank{2 + u % 2}")
+            for t in range(PACK):
+                nc.tensor.transpose(gates[u][:, t, :], turned[:, t * P : (t + 1) * P], identity[:])
 
         def hidden(u):
             cols = slice(u * CHUNK, (u + 1) * CHUNK)
+            if u < TURNED:
+                gate_view = gates[u][:].rearrange("p t j -> p j t")
+            else:
+                gate_view = gates[u][:].rearrange("p (j t) -> p j t", t=PACK)
             nc.vector.tensor_tensor(
                 z_bf[u % 2][:].rearrange("p (j t) -> p j t", t=PACK),
-                gates[u % 2][:].rearrange("p (j t) -> p j t", t=PACK),
+                gate_view,
                 y_gain[:, :, cols].rearrange("p t j -> p j t"),
                 ALU.mult,
             )
@@ -161,37 +198,45 @@ def tile_picked_mixingsumgthree_none_p_kernel(
         def second_layer(u):
             cols = slice(u * CHUNK, (u + 1) * CHUNK)
             for m in range(N // P):
-                product(h_bank[m][:, cols], w2_mx, slice(m * P, (m + 1) * P), z_mx, cols, u == 0, u == CHUNKS - 1)
+                product(h_bank[m][:, cols], w2_mx, slice(m * P, (m + 1) * P), z_mx, cols, u == 0, False)
 
         def side_weights(a):
-            w3_bf = members[a][:, 0, :].bitcast(BF16)
+            w3_bf = sums[CHUNKS - 2 + a][:].bitcast(BF16)
             dst, src = interleave_views(w3_bf, w3_raw[:, :, a * N // 2 : (a + 1) * N // 2])
             nc.scalar.copy(out=dst, in_=src)
             quantize(w3_mx[a], slice(0, N // 2), w3_bf)
 
-        for u in range(CHUNKS):
-            for t in range(PACK):
-                fetch_members(u, t)
-            if u == 0:
-                for t in range(PACK):
-                    nc.vector.tensor_scalar(y_gain[:, t, :], y[t][:, :S], gain[:, t : t + 1], None, ALU.mult)
-            if u == 1:
-                w2_bf = keep.tile([P, N * PACK], BF16, name="w2_bf", align_bytes=64)
-                dst, src = interleave_views(w2_bf[:], w2_raw[:])
-                nc.vector.tensor_copy(out=dst, in_=src)
-                w3_raw = load_weight(w3, "w3_raw")
-                quantize(w2_mx, slice(0, N), w2_bf[:])
-            if u > 0:
-                hidden(u - 1)
-                second_layer(u - 1)
-            add_pairs(u, 0)
-            add_pairs(u, 1)
-            gate(u)
-
-        last = slice(S - CHUNK, S)
+        fetch_members(0)
+        for t in range(PACK):
+            nc.vector.tensor_scalar(y_gain[:, t, :], y[t][:, :S], gain[:, t : t + 1], None, ALU.mult)
+        add_members(0)
+        fetch_members(1)
+        add_members(1)
+        w2_bf = keep.tile([P, N * PACK], BF16, name="w2_bf", align_bytes=64)
+        dst, src = interleave_views(w2_bf[:], w2_raw[:])
+        nc.vector.tensor_copy(out=dst, in_=src)
+        w3_raw = load_weight(w3, "w3_raw")
+        fetch_members(2)
+        quantize(w2_mx, slice(0, N), w2_bf[:])
+        gate(0)
+        turn_back(0)
+        gate(1)
+        turn_back(1)
+        hidden(0)
+        second_layer(0)
+        fetch_members(3)
+        add_members(2)
+        hidden(1)
+        second_layer(1)
+        add_members(3)
+        gate(2)
+        hidden(2)
+        second_layer(2)
         side_weights(0)
-        hidden(CHUNKS - 1)
+        gate(3)
+        hidden(3)
         side_weights(1)
+        last = slice(S - CHUNK, S)
         for m in range(N // P):
             for cols in (slice(0, 256), slice(256, 384), last):
                 product(h_bank[m][:, cols], w3_mx[m // 2], slice((m % 2) * P, (m % 2 + 1) * P), x_two, cols, False, False)

@@ -24,7 +24,7 @@ CHUNK = 128
 CHUNKS = S // CHUNK
 SCALAR_COLS = 24
 TURNED = 2
-VECTOR_PLANES = (2, 2, 1, 1)
+VECTOR_PLANES = 0
 
 
 def tile_picked_mixingsumgthree_none_p_kernel(
@@ -40,9 +40,9 @@ def tile_picked_mixingsumgthree_none_p_kernel(
             nc.sync.dma_start(tile[:], src)
             return tile
 
-        def load_weight(src, name):
-            tile = keep.tile([P, PACK, src.shape[1]], F32, name=name, tag="weight_raw")
-            nc.sync.dma_start(out=tile[:], in_=src.rearrange("(p j) c -> p j c", j=PACK))
+        def load_weight(src, name, queue=nc.sync):
+            tile = keep.tile([P, PACK, src.shape[1]], F32, name=name)
+            queue.dma_start(out=tile[:], in_=src.rearrange("(p j) c -> p j c", j=PACK))
             return tile
 
         def gather(on_vector, dst, window, offsets):
@@ -93,6 +93,8 @@ def tile_picked_mixingsumgthree_none_p_kernel(
         n1_sb = load_list(n1, "n1_sb")
         gain = keep.tile([P, PACK], F32, name="gain")
         nc.sync.dma_start(out=gain[:], in_=gn.rearrange("(p t) o -> p (t o)", t=PACK))
+        w3_raw = load_weight(w3, "w3_raw")
+        w2_raw = load_weight(w2, "w2_raw")
         n2_sb = load_list(n2, "n2_sb")
         n3_sb = load_list(n3, "n3_sb")
         n4_sb = load_list(n4, "n4_sb")
@@ -111,7 +113,6 @@ def tile_picked_mixingsumgthree_none_p_kernel(
                 out=w1_bf[a][:].rearrange("p (t m j) -> p m j t", t=2, j=PACK),
                 in_=w1_view[:, :, :, 2 * a : 2 * a + 2],
             )
-        w2_raw = load_weight(w2, "w2_raw")
         x_one = mx_tiles("x_one", S)
         x_two = mx_tiles("x_two", S)
         nc.vector.tensor_copy(x_one[1][:], table_scales[:].indirect(offs_sb[:]))
@@ -132,7 +133,7 @@ def tile_picked_mixingsumgthree_none_p_kernel(
             y.append(y_t)
 
         w2_mx = mx_tiles("w2", N)
-        w3_mx = [mx_tiles(f"w3_{a}", N // 2) for a in range(2)]
+        w3_mx = mx_tiles("w3", N)
         z_mx = mx_tiles("z", S)
         h_bank = [psum.tile([P, S], F32, name=f"h_bank{m}") for m in range(N // P)]
         members = [keep.tile([P, PACK, MEMBERS * CHUNK], F32, name=f"members{u}") for u in range(CHUNKS)]
@@ -141,106 +142,103 @@ def tile_picked_mixingsumgthree_none_p_kernel(
         gates = {}
         z_bf = [keep.tile([P, CHUNK * PACK], BF16, name=f"z_bf{b}", align_bytes=64) for b in range(2)]
 
-        def fetch_members(u):
-            cols = MEMBERS * CHUNK // 16
+        def fetch_members(u, js, planes_on_vector):
+            entries = slice(MEMBERS * js.start, MEMBERS * js.stop)
+            first = MEMBERS * CHUNK * u
+            cols = slice((first + entries.start) // 16, (first + entries.stop) // 16)
             for t in range(PACK):
-                on_vector = t >= PACK - VECTOR_PLANES[u]
-                gather(on_vector, members[u][:, t, :], y[t][:], n1_sb[:, u * cols : (u + 1) * cols])
+                on_vector = t >= PACK - planes_on_vector
+                gather(on_vector, members[u][:, t, entries], y[t][:], n1_sb[:, cols])
 
-        def add_members(u):
-            if u < TURNED:
-                sums[u] = psum.tile([P, PACK * P], F32, name=f"sums{u}", tag=f"bank{u % 2}")
-                for t in range(PACK):
-                    for s in range(MEMBERS):
-                        nc.tensor.matmul(
-                            sums[u][:, t * P : (t + 1) * P],
-                            members[u][:, t, s::MEMBERS],
-                            identity[:],
-                            start=s == 0,
-                            stop=s == MEMBERS - 1,
-                            is_transpose=True,
-                        )
-            else:
-                view = members[u][:].rearrange("p t (j s e) -> p j t s e", s=2, e=2)
-                for a in range(2):
-                    planes = slice(2 * a, 2 * a + 2)
-                    nc.vector.tensor_tensor(
-                        pairs[:, :, planes, :], view[:, :, planes, 0, :], view[:, :, planes, 1, :], ALU.add
+        def add_turned(u):
+            sums[u] = psum.tile([P, PACK * P], F32, name=f"sums{u}", tag=f"bank{u % 2}")
+            for t in range(PACK):
+                for s in range(MEMBERS):
+                    nc.tensor.matmul(
+                        sums[u][:, t * P : (t + 1) * P],
+                        members[u][:, t, s::MEMBERS],
+                        identity[:],
+                        start=s == 0,
+                        stop=s == MEMBERS - 1,
+                        is_transpose=True,
                     )
-                sums[u] = keep.tile([P, CHUNK * PACK], F32, name=f"sums{u}", align_bytes=64)
-                view = pairs[:].rearrange("p j t e -> p (j t) e")
-                nc.vector.tensor_tensor(sums[u][:], view[:, :, 0], view[:, :, 1], ALU.add)
 
-        def gate(u):
-            gates[u] = keep.tile([P, CHUNK * PACK], F32, name=f"gates{u}", align_bytes=64)
-            nc.scalar.activation(gates[u][:], sums[u][:], ACT.Sigmoid)
-
-        def turn_back(u):
-            turned = gates[u]
-            gates[u] = psum.tile([P, PACK, CHUNK], F32, name=f"back{u}", tag=f"bank{2 + u % 2}")
+        def gate_turned(u):
+            turned = keep.tile([P, PACK * P], F32, name=f"turned{u}")
+            nc.scalar.activation(turned[:], sums[u][:], ACT.Sigmoid)
+            back = psum.tile([P, PACK, CHUNK], F32, name=f"back{u}", tag=f"bank{2 + u % 2}")
             for t in range(PACK):
-                nc.tensor.transpose(gates[u][:, t, :], turned[:, t * P : (t + 1) * P], identity[:])
+                nc.tensor.transpose(back[:, t, :], turned[:, t * P : (t + 1) * P], identity[:])
+            gates[u] = back[:].rearrange("p t j -> p j t")
 
-        def hidden(u):
-            cols = slice(u * CHUNK, (u + 1) * CHUNK)
-            if u < TURNED:
-                gate_view = gates[u][:].rearrange("p t j -> p j t")
-            else:
-                gate_view = gates[u][:].rearrange("p (j t) -> p j t", t=PACK)
+        def add_plain(u, js):
+            view = members[u][:].rearrange("p t (j s e) -> p j t s e", s=2, e=2)
+            for a in range(2):
+                planes = slice(2 * a, 2 * a + 2)
+                nc.vector.tensor_tensor(
+                    pairs[:, js, planes, :], view[:, js, planes, 0, :], view[:, js, planes, 1, :], ALU.add
+                )
+            nc.vector.tensor_tensor(sums[u][:, js, :], pairs[:, js, :, 0], pairs[:, js, :, 1], ALU.add)
+
+        def gate_plain(u, js):
+            nc.scalar.activation(gates[u][:, js, :], sums[u][:, js, :], ACT.Sigmoid)
+
+        def hidden(u, js):
+            cols = slice(u * CHUNK + js.start, u * CHUNK + js.stop)
+            z_view = z_bf[u % 2][:].rearrange("p (j t) -> p j t", t=PACK)
             nc.vector.tensor_tensor(
-                z_bf[u % 2][:].rearrange("p (j t) -> p j t", t=PACK),
-                gate_view,
-                y_gain[:, :, cols].rearrange("p t j -> p j t"),
-                ALU.mult,
+                z_view[:, js, :], gates[u][:, js, :], y_gain[:, :, cols].rearrange("p t j -> p j t"), ALU.mult
             )
-            quantize(z_mx, cols, z_bf[u % 2][:])
+            quantize(z_mx, cols, z_bf[u % 2][:, js.start * PACK : js.stop * PACK])
 
         def second_layer(u):
             cols = slice(u * CHUNK, (u + 1) * CHUNK)
             for m in range(N // P):
-                product(h_bank[m][:, cols], w2_mx, slice(m * P, (m + 1) * P), z_mx, cols, u == 0, False)
+                product(h_bank[m][:, cols], w2_mx, slice(m * P, (m + 1) * P), z_mx, cols, False, u == CHUNKS - 1)
 
-        def side_weights(a):
-            w3_bf = sums[CHUNKS - 2 + a][:].bitcast(BF16)
-            dst, src = interleave_views(w3_bf, w3_raw[:, :, a * N // 2 : (a + 1) * N // 2])
-            nc.scalar.copy(out=dst, in_=src)
-            quantize(w3_mx[a], slice(0, N // 2), w3_bf)
+        def round_weight(raw, name):
+            grouped = keep.tile([P, N * PACK], BF16, name=name, align_bytes=64)
+            dst, src = interleave_views(grouped[:], raw[:])
+            nc.gpsimd.tensor_scalar(dst, src, 1.0, 0.0, ALU.mult, ALU.add)
+            return grouped
 
-        fetch_members(0)
+        whole = slice(0, CHUNK)
+        halves = (slice(0, CHUNK // 2), slice(CHUNK // 2, CHUNK))
+        for u in range(TURNED, CHUNKS):
+            sums[u] = keep.tile([P, CHUNK, PACK], F32, name=f"sums{u}")
+            gates[u] = keep.tile([P, CHUNK, PACK], F32, name=f"gates{u}")
+
         for t in range(PACK):
-            nc.vector.tensor_scalar(y_gain[:, t, :], y[t][:, :S], gain[:, t : t + 1], None, ALU.mult)
-        add_members(0)
-        fetch_members(1)
-        add_members(1)
-        w2_bf = keep.tile([P, N * PACK], BF16, name="w2_bf", align_bytes=64)
-        dst, src = interleave_views(w2_bf[:], w2_raw[:])
-        nc.vector.tensor_copy(out=dst, in_=src)
-        w3_raw = load_weight(w3, "w3_raw")
-        fetch_members(2)
+            nc.gpsimd.tensor_scalar(y_gain[:, t, :], y[t][:, :S], gain[:, t : t + 1], 0.0, ALU.mult, ALU.add)
+        w3_bf = round_weight(w3_raw, "w3_bf")
+        w2_bf = round_weight(w2_raw, "w2_bf")
+        for u in range(TURNED):
+            fetch_members(u, whole, 2)
+            add_turned(u)
+        fetch_members(2, whole, 2)
+        gate_turned(0)
+        quantize(w3_mx, slice(0, N), w3_bf[:])
         quantize(w2_mx, slice(0, N), w2_bf[:])
-        gate(0)
-        turn_back(0)
-        gate(1)
-        turn_back(1)
-        hidden(0)
-        second_layer(0)
-        fetch_members(3)
-        add_members(2)
-        hidden(1)
-        second_layer(1)
-        add_members(3)
-        gate(2)
-        hidden(2)
-        second_layer(2)
-        side_weights(0)
-        gate(3)
-        hidden(3)
-        side_weights(1)
-        last = slice(S - CHUNK, S)
+        add_plain(2, whole)
+        fetch_members(3, halves[0], 1)
+        gate_turned(1)
+        gate_plain(2, whole)
         for m in range(N // P):
-            for cols in (slice(0, 256), slice(256, 384), last):
-                product(h_bank[m][:, cols], w3_mx[m // 2], slice((m % 2) * P, (m % 2 + 1) * P), x_two, cols, False, False)
-            product(h_bank[m][:, last], w2_mx, slice(m * P, (m + 1) * P), z_mx, last, False, True)
+            product(h_bank[m][:], w3_mx, slice(m * P, (m + 1) * P), x_two, slice(0, S), True, False)
+        fetch_members(3, halves[1], 0)
+        hidden(0, whole)
+        second_layer(0)
+        add_plain(3, halves[0])
+        hidden(1, whole)
+        second_layer(1)
+        gate_plain(3, halves[0])
+        hidden(2, whole)
+        second_layer(2)
+        add_plain(3, halves[1])
+        hidden(3, halves[0])
+        gate_plain(3, halves[1])
+        hidden(3, halves[1])
+        second_layer(3)
 
         tiles = range(N // P)
         h = [keep.tile([P, S], F32, name=f"h{m}") for m in tiles]
@@ -249,10 +247,10 @@ def tile_picked_mixingsumgthree_none_p_kernel(
         picked = [keep.tile([P, S], F32, name=f"picked{m}") for m in tiles]
         result = [keep.tile([P, S], F32, name=f"result{m}") for m in tiles]
 
-        def gather_split(m, window, offsets):
-            cut = 16 * SCALAR_COLS
-            gather(False, picked[m][:, :cut], window[:], offsets[:, :SCALAR_COLS])
-            gather(True, picked[m][:, cut:], window[:], offsets[:, SCALAR_COLS:])
+        def gather_split(m, window, offsets, cols=SCALAR_COLS):
+            cut = 16 * cols
+            gather(False, picked[m][:, :cut], window[:], offsets[:, :cols])
+            gather(True, picked[m][:, cut:], window[:], offsets[:, cols:])
 
         for m in tiles:
             copy = nc.vector.tensor_copy if m % 2 else nc.scalar.copy
@@ -264,6 +262,6 @@ def tile_picked_mixingsumgthree_none_p_kernel(
             gather_split(m, st[m], n3_sb)
             nc.vector.tensor_tensor(su[m][:], st[m][:], picked[m][:], ALU.max)
         for m in tiles:
-            gather_split(m, su[m], n4_sb)
+            gather_split(m, su[m], n4_sb, 24)
             nc.vector.scalar_tensor_tensor(result[m][:], picked[m][:], 0.5, su[m][:], ALU.mult, ALU.add)
             nc.sync.dma_start(out=out[m * P : (m + 1) * P, :], in_=result[m][:])

@@ -137,7 +137,7 @@ def tile_picked_mixingsumgthree_none_p_kernel(
         z_mx = mx_tiles("z", S)
         h_bank = [psum.tile([P, S], F32, name=f"h_bank{m}") for m in range(N // P)]
         members = [keep.tile([P, PACK, MEMBERS * CHUNK], F32, name=f"members{u}") for u in range(CHUNKS)]
-        pairs = keep.tile([P, CHUNK, PACK, 2], F32, name="pairs")
+        pairs = {}
         sums = {}
         gates = {}
         z_bf = [keep.tile([P, CHUNK * PACK], BF16, name=f"z_bf{b}", align_bytes=64) for b in range(2)]
@@ -169,27 +169,30 @@ def tile_picked_mixingsumgthree_none_p_kernel(
             back = psum.tile([P, PACK, CHUNK], F32, name=f"back{u}", tag=f"bank{2 + u % 2}")
             for t in range(PACK):
                 nc.tensor.transpose(back[:, t, :], turned[:, t * P : (t + 1) * P], identity[:])
-            gates[u] = back[:].rearrange("p t j -> p j t")
+            gates[u] = back
 
-        def add_plain(u, js):
-            view = members[u][:].rearrange("p t (j s e) -> p j t s e", s=2, e=2)
+        def add_plain(u, js, engine):
+            view = members[u][:].rearrange("p t (j s e) -> p t j s e", s=2, e=2)
             for a in range(2):
                 planes = slice(2 * a, 2 * a + 2)
-                nc.vector.tensor_tensor(
-                    pairs[:, js, planes, :], view[:, js, planes, 0, :], view[:, js, planes, 1, :], ALU.add
+                engine.tensor_tensor(
+                    pairs[u][:, planes, js, :], view[:, planes, js, 0, :], view[:, planes, js, 1, :], ALU.add
                 )
-            nc.vector.tensor_tensor(sums[u][:, js, :], pairs[:, js, :, 0], pairs[:, js, :, 1], ALU.add)
+            engine.tensor_tensor(sums[u][:, :, js], pairs[u][:, :, js, 0], pairs[u][:, :, js, 1], ALU.add)
 
         def gate_plain(u, js):
-            nc.scalar.activation(gates[u][:, js, :], sums[u][:, js, :], ACT.Sigmoid)
+            nc.scalar.activation(gates[u][:, :, js], sums[u][:, :, js], ACT.Sigmoid)
 
         def hidden(u, js):
             cols = slice(u * CHUNK + js.start, u * CHUNK + js.stop)
-            z_view = z_bf[u % 2][:].rearrange("p (j t) -> p j t", t=PACK)
+            grouped = z_bf[u % 2][:, js.start * PACK : js.stop * PACK]
             nc.vector.tensor_tensor(
-                z_view[:, js, :], gates[u][:, js, :], y_gain[:, :, cols].rearrange("p t j -> p j t"), ALU.mult
+                grouped.rearrange("p (c i t) -> p c t i", i=4, t=PACK),
+                gates[u][:, :, js].rearrange("p t (c i) -> p c t i", i=4),
+                y_gain[:, :, cols].rearrange("p t (c i) -> p c t i", i=4),
+                ALU.mult,
             )
-            quantize(z_mx, cols, z_bf[u % 2][:, js.start * PACK : js.stop * PACK])
+            quantize(z_mx, cols, grouped)
 
         def second_layer(u):
             cols = slice(u * CHUNK, (u + 1) * CHUNK)
@@ -198,15 +201,16 @@ def tile_picked_mixingsumgthree_none_p_kernel(
 
         def round_weight(raw, name):
             grouped = keep.tile([P, N * PACK], BF16, name=name, align_bytes=64)
-            dst, src = interleave_views(grouped[:], raw[:])
-            nc.gpsimd.tensor_scalar(dst, src, 1.0, 0.0, ALU.mult, ALU.add)
+            dst = grouped[:].rearrange("p (c j) -> p c j", j=PACK)
+            nc.gpsimd.tensor_scalar(dst, raw[:].rearrange("p j c -> p c j"), 1.0, 0.0, ALU.mult, ALU.add)
             return grouped
 
         whole = slice(0, CHUNK)
         halves = (slice(0, CHUNK // 2), slice(CHUNK // 2, CHUNK))
         for u in range(TURNED, CHUNKS):
-            sums[u] = keep.tile([P, CHUNK, PACK], F32, name=f"sums{u}")
-            gates[u] = keep.tile([P, CHUNK, PACK], F32, name=f"gates{u}")
+            pairs[u] = keep.tile([P, PACK, CHUNK, 2], F32, name=f"pairs{u}")
+            sums[u] = keep.tile([P, PACK, CHUNK], F32, name=f"sums{u}")
+            gates[u] = keep.tile([P, PACK, CHUNK], F32, name=f"gates{u}")
 
         for t in range(PACK):
             nc.gpsimd.tensor_scalar(y_gain[:, t, :], y[t][:, :S], gain[:, t : t + 1], 0.0, ALU.mult, ALU.add)
@@ -219,7 +223,7 @@ def tile_picked_mixingsumgthree_none_p_kernel(
         gate_turned(0)
         quantize(w3_mx, slice(0, N), w3_bf[:])
         quantize(w2_mx, slice(0, N), w2_bf[:])
-        add_plain(2, whole)
+        add_plain(2, whole, nc.vector)
         fetch_members(3, halves[0], 1)
         gate_turned(1)
         gate_plain(2, whole)
@@ -228,13 +232,13 @@ def tile_picked_mixingsumgthree_none_p_kernel(
         fetch_members(3, halves[1], 0)
         hidden(0, whole)
         second_layer(0)
-        add_plain(3, halves[0])
+        add_plain(3, halves[0], nc.vector)
         hidden(1, whole)
         second_layer(1)
         gate_plain(3, halves[0])
         hidden(2, whole)
         second_layer(2)
-        add_plain(3, halves[1])
+        add_plain(3, halves[1], nc.vector)
         hidden(3, halves[0])
         gate_plain(3, halves[1])
         hidden(3, halves[1])
@@ -263,5 +267,9 @@ def tile_picked_mixingsumgthree_none_p_kernel(
             nc.vector.tensor_tensor(su[m][:], st[m][:], picked[m][:], ALU.max)
         for m in tiles:
             gather_split(m, su[m], n4_sb, 24)
-            nc.vector.scalar_tensor_tensor(result[m][:], picked[m][:], 0.5, su[m][:], ALU.mult, ALU.add)
-            nc.sync.dma_start(out=out[m * P : (m + 1) * P, :], in_=result[m][:])
+            pieces = (slice(0, S // 2), slice(S // 2, S)) if m == tiles[-1] else (slice(0, S),)
+            for cols in pieces:
+                nc.vector.scalar_tensor_tensor(
+                    result[m][:, cols], picked[m][:, cols], 0.5, su[m][:, cols], ALU.mult, ALU.add
+                )
+                nc.sync.dma_start(out=out[m * P : (m + 1) * P, cols], in_=result[m][:, cols])

@@ -18,13 +18,20 @@ ACT = mybir.ActivationFunctionType
 
 P = 128
 PACK = 4
+LANES = 16
+QUADRANT = 32
 MEMBERS = 4
-WINDOW = S + 16
 CHUNK = 128
 CHUNKS = S // CHUNK
-SCALAR_COLS = 24
 TURNED = 2
-VECTOR_PLANES = 0
+EARLY = S - CHUNK
+ROW_TILES = N // P
+assert TURNED == 2 and CHUNKS == 4
+Y_WINDOW = S + LANES
+VECTOR_PLANES_TURNED = 2
+VECTOR_PLANES_PLAIN = 1
+SCALAR_COLS = 24
+SCALAR_COLS_FIRST = 22
 
 
 def tile_picked_mixingsumgthree_none_p_kernel(
@@ -35,14 +42,17 @@ def tile_picked_mixingsumgthree_none_p_kernel(
         keep = ctx.enter_context(tc.tile_pool(name="keep", bufs=1))
         psum = ctx.enter_context(tc.psum_pool(name="psum", bufs=1))
 
+        def block(index, width):
+            return slice(index * width, (index + 1) * width)
+
         def load_list(src, name):
             tile = keep.tile(list(src.shape), U16, name=name)
             nc.sync.dma_start(tile[:], src)
             return tile
 
-        def load_weight(src, name, queue=nc.sync):
+        def load_weight(src, name):
             tile = keep.tile([P, PACK, src.shape[1]], F32, name=name)
-            queue.dma_start(out=tile[:], in_=src.rearrange("(p j) c -> p j c", j=PACK))
+            nc.sync.dma_start(out=tile[:], in_=src.rearrange("(p j) c -> p j c", j=PACK))
             return tile
 
         def gather(on_vector, dst, window, offsets):
@@ -51,13 +61,14 @@ def tile_picked_mixingsumgthree_none_p_kernel(
             else:
                 nc.scalar.activation(dst, window.indirect(offsets), ACT.Copy)
 
-        def mx_tiles(name, width, tag=""):
-            codes = keep.tile([P, width], U32, name=name + "_codes", tag=tag, align_bytes=64)
+        def mx_tiles(name, width):
+            words = keep.tile([P, width], U32, name=name + "_words", align_bytes=64)
             scales = keep.tile([P, width], U8, name=name + "_scales", align_bytes=64)
-            return codes, scales
+            return words, scales
 
-        def quantize(mx, cols, src):
-            nc.vector.quantize_mx(out=mx[0][:, cols].bitcast(FP8X4), scales=mx[1][:, cols], in_=src)
+        def quantize(mx, cols, grouped):
+            words, scales = mx
+            nc.vector.quantize_mx(out=words[:, cols].bitcast(FP8X4), scales=scales[:, cols], in_=grouped)
 
         def product(dst, lhs, lhs_cols, rhs, rhs_cols, start, stop):
             nc.tensor.matmul_mx(
@@ -70,19 +81,13 @@ def tile_picked_mixingsumgthree_none_p_kernel(
                 stop=stop,
             )
 
-        def interleave_views(grouped, raw):
-            return (
-                grouped.rearrange("p (c i j) -> p c j i", i=4, j=PACK),
-                raw.rearrange("p j (c i) -> p c j i", i=4),
-            )
-
         table_scales = keep.tile([P, T], U8, name="table_scales")
         nc.gpsimd.memset(table_scales[:].bitcast(I32), 0)
         offs_sb = load_list(offs, "offs_sb")
         two_sb = load_list(two, "two_sb")
         for r in range(4):
             nc.sync.dma_start(
-                out=table_scales[r:P:32, :].bitcast(I32), in_=x_scales[0, r:16:4, :].bitcast(I32)
+                out=table_scales[r:P:QUADRANT, :].bitcast(I32), in_=x_scales[0, r::4, :].bitcast(I32)
             )
         w1_raw = load_weight(w1, "w1_raw")
         table_words = keep.tile([P, T], U32, name="table_words")
@@ -102,60 +107,65 @@ def tile_picked_mixingsumgthree_none_p_kernel(
         identity = keep.tile([P, P], F32, name="identity")
         make_identity(nc, identity[:])
 
+        warm = keep.tile([P, 1], F32, name="warm")
+        nc.scalar.activation(warm[:], identity[:, 0:1], ACT.Sigmoid)
+
         w1_mx = [mx_tiles(f"w1_{a}", 2 * P) for a in range(2)]
-        w1_bf = [
-            keep.tile([P, 2 * P * PACK], BF16, name=f"w1_bf{a}", tag=f"w1_bf{a}", align_bytes=64) for a in range(2)
-        ]
+        w1_bf = [keep.tile([P, 2 * P * PACK], BF16, name=f"w1_bf{a}", align_bytes=64) for a in range(2)]
         w1_view = w1_raw[:].rearrange("p j (m t) -> p m j t", t=PACK)
-        for a in range(2):
-            copy = nc.vector.tensor_copy if a == 0 else nc.scalar.copy
+        for a, copy in enumerate((nc.vector.tensor_copy, nc.scalar.copy)):
             copy(
                 out=w1_bf[a][:].rearrange("p (t m j) -> p m j t", t=2, j=PACK),
-                in_=w1_view[:, :, :, 2 * a : 2 * a + 2],
+                in_=w1_view[:, :, :, block(a, 2)],
             )
+
         x_one = mx_tiles("x_one", S)
         x_two = mx_tiles("x_two", S)
         nc.vector.tensor_copy(x_one[1][:], table_scales[:].indirect(offs_sb[:]))
         nc.vector.tensor_copy(x_two[1][:], table_scales[:].indirect(two_sb[:]))
-        quantize(w1_mx[0], slice(0, 2 * P), w1_bf[0][:])
-        quantize(w1_mx[1], slice(0, 2 * P), w1_bf[1][:])
-        nc.vector.tensor_copy(x_one[0][:], table_words[:].indirect(offs_sb[:]))
+        for a in range(2):
+            quantize(w1_mx[a], slice(0, 2 * P), w1_bf[a][:])
+        for a in range(2):
+            nc.vector.tensor_copy(
+                x_one[0][:, block(a, S // 2)], table_words[:].indirect(offs_sb[:, block(a, S // 2 // LANES)])
+            )
         nc.vector.tensor_copy(x_two[0][:], table_words[:].indirect(two_sb[:]))
 
         y = []
         y_gain = keep.tile([P, PACK, S], F32, name="y_gain")
         for t in range(PACK):
             bank = psum.tile([P, S], F32, name=f"y_bank{t}", tag=f"bank{t}")
-            product(bank[:], w1_mx[t // 2], slice(P * (t % 2), P * (t % 2 + 1)), x_one, slice(0, S), True, True)
-            y_t = keep.tile([P, WINDOW], F32, name=f"y{t}")
+            for a in range(2):
+                cols = block(a, S // 2)
+                product(bank[:, cols], w1_mx[t // 2], block(t % 2, P), x_one, cols, True, True)
+            plane = keep.tile([P, Y_WINDOW], F32, name=f"y{t}")
             copy = nc.vector.tensor_copy if t > 0 else nc.scalar.copy
-            copy(out=y_t[:, :S], in_=bank[:])
-            y.append(y_t)
+            copy(out=plane[:, :S], in_=bank[:])
+            y.append(plane)
 
         w2_mx = mx_tiles("w2", N)
         w3_mx = mx_tiles("w3", N)
         z_mx = mx_tiles("z", S)
-        h_bank = [psum.tile([P, S], F32, name=f"h_bank{m}") for m in range(N // P)]
+        h_early = [psum.tile([P, EARLY], F32, name=f"h_early{m}") for m in range(ROW_TILES)]
         members = [keep.tile([P, PACK, MEMBERS * CHUNK], F32, name=f"members{u}") for u in range(CHUNKS)]
+        z_bf = [keep.tile([P, CHUNK * PACK], BF16, name=f"z_bf{u}", align_bytes=64) for u in range(CHUNKS)]
         pairs = {}
         sums = {}
         gates = {}
-        z_bf = [keep.tile([P, CHUNK * PACK], BF16, name=f"z_bf{b}", align_bytes=64) for b in range(2)]
 
-        def fetch_members(u, js, planes_on_vector):
-            entries = slice(MEMBERS * js.start, MEMBERS * js.stop)
+        def fetch_members(u, places, vector_planes):
+            entries = slice(MEMBERS * places.start, MEMBERS * places.stop)
             first = MEMBERS * CHUNK * u
-            cols = slice((first + entries.start) // 16, (first + entries.stop) // 16)
+            cols = slice((first + entries.start) // LANES, (first + entries.stop) // LANES)
             for t in range(PACK):
-                on_vector = t >= PACK - planes_on_vector
-                gather(on_vector, members[u][:, t, entries], y[t][:], n1_sb[:, cols])
+                gather(t >= PACK - vector_planes, members[u][:, t, entries], y[t][:], n1_sb[:, cols])
 
         def add_turned(u):
-            sums[u] = psum.tile([P, PACK * P], F32, name=f"sums{u}", tag=f"bank{u % 2}")
+            sums[u] = psum.tile([P, PACK * P], F32, name=f"sums{u}", tag=f"bank{u}")
             for t in range(PACK):
                 for s in range(MEMBERS):
                     nc.tensor.matmul(
-                        sums[u][:, t * P : (t + 1) * P],
+                        sums[u][:, block(t, P)],
                         members[u][:, t, s::MEMBERS],
                         identity[:],
                         start=s == 0,
@@ -166,38 +176,41 @@ def tile_picked_mixingsumgthree_none_p_kernel(
         def gate_turned(u):
             turned = keep.tile([P, PACK * P], F32, name=f"turned{u}")
             nc.scalar.activation(turned[:], sums[u][:], ACT.Sigmoid)
-            back = psum.tile([P, PACK, CHUNK], F32, name=f"back{u}", tag=f"bank{2 + u % 2}")
+            gates[u] = psum.tile([P, PACK, CHUNK], F32, name=f"gates{u}", tag=f"bank{TURNED + u}")
             for t in range(PACK):
-                nc.tensor.transpose(back[:, t, :], turned[:, t * P : (t + 1) * P], identity[:])
-            gates[u] = back
+                nc.tensor.transpose(gates[u][:, t, :], turned[:, block(t, P)], identity[:])
 
-        def add_plain(u, js, engine):
+        def add_plain(u, places):
             view = members[u][:].rearrange("p t (j s e) -> p t j s e", s=2, e=2)
             for a in range(2):
-                planes = slice(2 * a, 2 * a + 2)
-                engine.tensor_tensor(
-                    pairs[u][:, planes, js, :], view[:, planes, js, 0, :], view[:, planes, js, 1, :], ALU.add
+                planes = block(a, 2)
+                nc.vector.tensor_tensor(
+                    pairs[u][:, planes, places, :], view[:, planes, places, 0, :], view[:, planes, places, 1, :], ALU.add
                 )
-            engine.tensor_tensor(sums[u][:, :, js], pairs[u][:, :, js, 0], pairs[u][:, :, js, 1], ALU.add)
+            nc.vector.tensor_tensor(sums[u][:, :, places], pairs[u][:, :, places, 0], pairs[u][:, :, places, 1], ALU.add)
 
-        def gate_plain(u, js):
-            nc.scalar.activation(gates[u][:, :, js], sums[u][:, :, js], ACT.Sigmoid)
+        def gate_plain(u, places):
+            nc.scalar.activation(gates[u][:, :, places], sums[u][:, :, places], ACT.Sigmoid)
 
-        def hidden(u, js):
-            cols = slice(u * CHUNK + js.start, u * CHUNK + js.stop)
-            grouped = z_bf[u % 2][:, js.start * PACK : js.stop * PACK]
+        def hidden(u, places):
+            cols = slice(u * CHUNK + places.start, u * CHUNK + places.stop)
+            grouped = z_bf[u][:, places.start * PACK : places.stop * PACK]
             nc.vector.tensor_tensor(
                 grouped.rearrange("p (c i t) -> p c t i", i=4, t=PACK),
-                gates[u][:, :, js].rearrange("p t (c i) -> p c t i", i=4),
+                gates[u][:, :, places].rearrange("p t (c i) -> p c t i", i=4),
                 y_gain[:, :, cols].rearrange("p t (c i) -> p c t i", i=4),
                 ALU.mult,
             )
             quantize(z_mx, cols, grouped)
 
         def second_layer(u):
-            cols = slice(u * CHUNK, (u + 1) * CHUNK)
-            for m in range(N // P):
-                product(h_bank[m][:, cols], w2_mx, slice(m * P, (m + 1) * P), z_mx, cols, False, u == CHUNKS - 1)
+            cols = block(u, CHUNK)
+            for m in range(ROW_TILES):
+                if u < CHUNKS - 1:
+                    dst, stop = h_early[m][:, cols], u == CHUNKS - 2
+                else:
+                    dst, stop = h_last[m // 2][:, m % 2, :], m % 2 == 1
+                product(dst, w2_mx, block(m, P), z_mx, cols, False, stop)
 
         def round_weight(raw, name):
             grouped = keep.tile([P, N * PACK], BF16, name=name, align_bytes=64)
@@ -205,71 +218,83 @@ def tile_picked_mixingsumgthree_none_p_kernel(
             nc.gpsimd.tensor_scalar(dst, raw[:].rearrange("p j c -> p c j"), 1.0, 0.0, ALU.mult, ALU.add)
             return grouped
 
+        third, last = CHUNKS - 2, CHUNKS - 1
         whole = slice(0, CHUNK)
-        halves = (slice(0, CHUNK // 2), slice(CHUNK // 2, CHUNK))
-        for u in range(TURNED, CHUNKS):
-            pairs[u] = keep.tile([P, PACK, CHUNK, 2], F32, name=f"pairs{u}")
-            sums[u] = keep.tile([P, PACK, CHUNK], F32, name=f"sums{u}")
-            gates[u] = keep.tile([P, PACK, CHUNK], F32, name=f"gates{u}")
+        halves = [block(a, CHUNK // 2) for a in range(2)]
+        for u in (third, last):
+            pairs[u] = keep.tile([P, PACK, CHUNK, 2], F32, name=f"pairs{u}", tag=f"pairs{u}", align_bytes=64)
+            gates[u] = keep.tile([P, PACK, CHUNK], F32, name=f"gates{u}", tag=f"gates{u}", align_bytes=64)
+        sums[third] = members[last][:, :, 2 * CHUNK : 3 * CHUNK]
+        sums[last] = keep.tile([P, PACK, CHUNK], F32, name="sums_last", tag="sums_last", align_bytes=64)
 
         for t in range(PACK):
             nc.gpsimd.tensor_scalar(y_gain[:, t, :], y[t][:, :S], gain[:, t : t + 1], 0.0, ALU.mult, ALU.add)
         w3_bf = round_weight(w3_raw, "w3_bf")
         w2_bf = round_weight(w2_raw, "w2_bf")
+
         for u in range(TURNED):
-            fetch_members(u, whole, 2)
+            fetch_members(u, whole, VECTOR_PLANES_TURNED)
             add_turned(u)
-        fetch_members(2, whole, 2)
+        fetch_members(third, whole, VECTOR_PLANES_PLAIN)
         gate_turned(0)
         quantize(w3_mx, slice(0, N), w3_bf[:])
         quantize(w2_mx, slice(0, N), w2_bf[:])
-        add_plain(2, whole, nc.vector)
-        fetch_members(3, halves[0], 1)
+        add_plain(third, whole)
+        fetch_members(last, halves[0], VECTOR_PLANES_PLAIN)
         gate_turned(1)
-        gate_plain(2, whole)
-        for m in range(N // P):
-            product(h_bank[m][:], w3_mx, slice(m * P, (m + 1) * P), x_two, slice(0, S), True, False)
-        fetch_members(3, halves[1], 0)
+        gate_plain(third, whole)
+
+        h_last = [psum.tile([P, 2, CHUNK], F32, name=f"h_last{a}", tag=f"bank{a}") for a in range(2)]
+        for m in range(ROW_TILES):
+            rows = block(m, P)
+            product(h_early[m][:, : 2 * CHUNK], w3_mx, rows, x_two, slice(0, 2 * CHUNK), True, False)
+            product(h_early[m][:, 2 * CHUNK :], w3_mx, rows, x_two, block(third, CHUNK), False, False)
+            product(h_last[m // 2][:, m % 2, :], w3_mx, rows, x_two, block(last, CHUNK), m % 2 == 0, False)
+
         hidden(0, whole)
         second_layer(0)
-        add_plain(3, halves[0], nc.vector)
-        hidden(1, whole)
-        second_layer(1)
-        gate_plain(3, halves[0])
-        hidden(2, whole)
-        second_layer(2)
-        add_plain(3, halves[1], nc.vector)
-        hidden(3, halves[0])
-        gate_plain(3, halves[1])
-        hidden(3, halves[1])
-        second_layer(3)
+        add_plain(last, halves[0])
+        gate_plain(last, halves[0])
+        fetch_members(last, halves[1], 0)
+        for u in (1, third):
+            hidden(u, whole)
+            second_layer(u)
+        add_plain(last, halves[1])
+        hidden(last, halves[0])
+        gate_plain(last, halves[1])
+        hidden(last, halves[1])
+        second_layer(last)
 
-        tiles = range(N // P)
-        h = [keep.tile([P, S], F32, name=f"h{m}") for m in tiles]
+        tiles = range(ROW_TILES)
+        h_tags = ("h0", "sums_last", f"pairs{last}", f"gates{last}")
+        h = [keep.tile([P, S], F32, name=f"h{m}", tag=h_tags[m], align_bytes=64) for m in tiles]
         st = [keep.tile([P, S], F32, name=f"st{m}") for m in tiles]
         su = [keep.tile([P, S], F32, name=f"su{m}") for m in tiles]
         picked = [keep.tile([P, S], F32, name=f"picked{m}") for m in tiles]
         result = [keep.tile([P, S], F32, name=f"result{m}") for m in tiles]
 
-        def gather_split(m, window, offsets, cols=SCALAR_COLS):
-            cut = 16 * cols
-            gather(False, picked[m][:, :cut], window[:], offsets[:, :cols])
-            gather(True, picked[m][:, cut:], window[:], offsets[:, cols:])
+        def gather_shared(m, window, offsets, scalar_cols):
+            cut = LANES * scalar_cols
+            gather(False, picked[m][:, :cut], window[:], offsets[:, :scalar_cols])
+            gather(True, picked[m][:, cut:], window[:], offsets[:, scalar_cols:])
 
         for m in tiles:
-            copy = nc.vector.tensor_copy if m % 2 else nc.scalar.copy
-            copy(out=h[m][:], in_=h_bank[m][:])
+            nc.scalar.copy(out=h[m][:, :EARLY], in_=h_early[m][:])
         for m in tiles:
-            gather_split(m, h[m], n2_sb)
-            nc.vector.tensor_tensor(st[m][:], h_bank[m][:], picked[m][:], ALU.subtract)
+            copy = nc.vector.tensor_copy if m // 2 else nc.scalar.copy
+            copy(out=h[m][:, EARLY:], in_=h_last[m // 2][:, m % 2, :])
         for m in tiles:
-            gather_split(m, st[m], n3_sb)
+            gather_shared(m, h[m], n2_sb, SCALAR_COLS_FIRST)
+            nc.vector.tensor_tensor(st[m][:], h[m][:], picked[m][:], ALU.subtract)
+        for m in tiles:
+            gather_shared(m, st[m], n3_sb, SCALAR_COLS)
             nc.vector.tensor_tensor(su[m][:], st[m][:], picked[m][:], ALU.max)
         for m in tiles:
-            gather_split(m, su[m], n4_sb, 24)
-            pieces = (slice(0, S // 2), slice(S // 2, S)) if m == tiles[-1] else (slice(0, S),)
-            for cols in pieces:
+            gather_shared(m, su[m], n4_sb, SCALAR_COLS)
+            pieces = 2 if m == ROW_TILES - 1 else 1
+            for a in range(pieces):
+                cols = block(a, S // pieces)
                 nc.vector.scalar_tensor_tensor(
                     result[m][:, cols], picked[m][:, cols], 0.5, su[m][:, cols], ALU.mult, ALU.add
                 )
-                nc.sync.dma_start(out=out[m * P : (m + 1) * P, cols], in_=result[m][:, cols])
+                nc.sync.dma_start(out=out[block(m, P), cols], in_=result[m][:, cols])

from contextlib import ExitStack

import concourse.mybir as mybir
from concourse.masks import make_identity

K, T, S, N, H = 512, 2048, 512, 512, 512
FLOPS = 2 * S * (K * H + H * N + K * N)

F32 = mybir.dt.float32
BF16 = mybir.dt.bfloat16
I32 = mybir.dt.int32
U32 = mybir.dt.uint32
U16 = mybir.dt.uint16
U8 = mybir.dt.uint8
FP8X4 = mybir.dt.float8_e4m3fn_x4
ALU = mybir.AluOpType
ACT = mybir.ActivationFunctionType

P = 128
PACK = 4
LANES = 16
QUADRANT = 32
MEMBERS = 4
CHUNK = 128
CHUNKS = S // CHUNK
TURNED = 2
EARLY = S - CHUNK
ROW_TILES = N // P
assert TURNED == 2 and CHUNKS == 4
Y_WINDOW = S + LANES
VECTOR_PLANES_TURNED = 2
VECTOR_PLANES_PLAIN = 1
SCALAR_COLS = 24
SCALAR_COLS_FIRST = 22


def tile_picked_mixingsumgthree_none_p_kernel(
    tc, x_words, x_scales, w1, gn, w2, w3, offs, n1, two, n2, n3, n4, out
):
    nc = tc.nc
    with ExitStack() as ctx:
        keep = ctx.enter_context(tc.tile_pool(name="keep", bufs=1))
        psum = ctx.enter_context(tc.psum_pool(name="psum", bufs=1))

        def block(index, width):
            return slice(index * width, (index + 1) * width)

        def load_list(src, name):
            tile = keep.tile(list(src.shape), U16, name=name)
            nc.sync.dma_start(tile[:], src)
            return tile

        def load_weight(src, name):
            tile = keep.tile([P, PACK, src.shape[1]], F32, name=name)
            nc.sync.dma_start(out=tile[:], in_=src.rearrange("(p j) c -> p j c", j=PACK))
            return tile

        def gather(on_vector, dst, window, offsets):
            if on_vector:
                nc.vector.tensor_copy(dst, window.indirect(offsets))
            else:
                nc.scalar.activation(dst, window.indirect(offsets), ACT.Copy)

        def mx_tiles(name, width):
            words = keep.tile([P, width], U32, name=name + "_words", align_bytes=64)
            scales = keep.tile([P, width], U8, name=name + "_scales", align_bytes=64)
            return words, scales

        def quantize(mx, cols, grouped):
            words, scales = mx
            nc.vector.quantize_mx(out=words[:, cols].bitcast(FP8X4), scales=scales[:, cols], in_=grouped)

        def product(dst, lhs, lhs_cols, rhs, rhs_cols, start, stop):
            nc.tensor.matmul_mx(
                out=dst,
                lhsT=lhs[0][:, lhs_cols].bitcast(FP8X4),
                lhsT_scale=lhs[1][:, lhs_cols],
                rhs=rhs[0][:, rhs_cols].bitcast(FP8X4),
                rhs_scale=rhs[1][:, rhs_cols],
                start=start,
                stop=stop,
            )

        table_scales = keep.tile([P, T], U8, name="table_scales")
        nc.gpsimd.memset(table_scales[:].bitcast(I32), 0)
        offs_sb = load_list(offs, "offs_sb")
        two_sb = load_list(two, "two_sb")
        for r in range(4):
            nc.sync.dma_start(
                out=table_scales[r:P:QUADRANT, :].bitcast(I32), in_=x_scales[0, r::4, :].bitcast(I32)
            )
        w1_raw = load_weight(w1, "w1_raw")
        table_words = keep.tile([P, T], U32, name="table_words")
        nc.sync.dma_start(
            out=table_words[:].bitcast(I32),
            in_=x_words[0].rearrange("p c r -> p (c r)").bitcast(I32),
        )
        n1_sb = load_list(n1, "n1_sb")
        gain = keep.tile([P, PACK], F32, name="gain")
        nc.sync.dma_start(out=gain[:], in_=gn.rearrange("(p t) o -> p (t o)", t=PACK))
        w3_raw = load_weight(w3, "w3_raw")
        w2_raw = load_weight(w2, "w2_raw")
        n2_sb = load_list(n2, "n2_sb")
        n3_sb = load_list(n3, "n3_sb")
        n4_sb = load_list(n4, "n4_sb")

        identity = keep.tile([P, P], F32, name="identity")
        make_identity(nc, identity[:])

        warm = keep.tile([P, 1], F32, name="warm")
        nc.scalar.activation(warm[:], identity[:, 0:1], ACT.Sigmoid)

        w1_mx = [mx_tiles(f"w1_{a}", 2 * P) for a in range(2)]
        w1_bf = [keep.tile([P, 2 * P * PACK], BF16, name=f"w1_bf{a}", align_bytes=64) for a in range(2)]
        w1_view = w1_raw[:].rearrange("p j (m t) -> p m j t", t=PACK)
        for a, copy in enumerate((nc.vector.tensor_copy, nc.scalar.copy)):
            copy(
                out=w1_bf[a][:].rearrange("p (t m j) -> p m j t", t=2, j=PACK),
                in_=w1_view[:, :, :, block(a, 2)],
            )

        x_one = mx_tiles("x_one", S)
        x_two = mx_tiles("x_two", S)
        nc.vector.tensor_copy(x_one[1][:], table_scales[:].indirect(offs_sb[:]))
        nc.vector.tensor_copy(x_two[1][:], table_scales[:].indirect(two_sb[:]))
        for a in range(2):
            quantize(w1_mx[a], slice(0, 2 * P), w1_bf[a][:])
        for a in range(2):
            nc.vector.tensor_copy(
                x_one[0][:, block(a, S // 2)], table_words[:].indirect(offs_sb[:, block(a, S // 2 // LANES)])
            )
        nc.vector.tensor_copy(x_two[0][:], table_words[:].indirect(two_sb[:]))

        y = []
        y_gain = keep.tile([P, PACK, S], F32, name="y_gain")
        for t in range(PACK):
            bank = psum.tile([P, S], F32, name=f"y_bank{t}", tag=f"bank{t}")
            for a in range(2):
                cols = block(a, S // 2)
                product(bank[:, cols], w1_mx[t // 2], block(t % 2, P), x_one, cols, True, True)
            plane = keep.tile([P, Y_WINDOW], F32, name=f"y{t}")
            copy = nc.vector.tensor_copy if t > 0 else nc.scalar.copy
            copy(out=plane[:, :S], in_=bank[:])
            y.append(plane)

        w2_mx = mx_tiles("w2", N)
        w3_mx = mx_tiles("w3", N)
        z_mx = mx_tiles("z", S)
        h_early = [psum.tile([P, EARLY], F32, name=f"h_early{m}") for m in range(ROW_TILES)]
        members = [keep.tile([P, PACK, MEMBERS * CHUNK], F32, name=f"members{u}") for u in range(CHUNKS)]
        z_bf = [keep.tile([P, CHUNK * PACK], BF16, name=f"z_bf{u}", align_bytes=64) for u in range(CHUNKS)]
        pairs = {}
        sums = {}
        gates = {}

        def fetch_members(u, places, vector_planes):
            entries = slice(MEMBERS * places.start, MEMBERS * places.stop)
            first = MEMBERS * CHUNK * u
            cols = slice((first + entries.start) // LANES, (first + entries.stop) // LANES)
            for t in range(PACK):
                gather(t >= PACK - vector_planes, members[u][:, t, entries], y[t][:], n1_sb[:, cols])

        def add_turned(u):
            sums[u] = psum.tile([P, PACK * P], F32, name=f"sums{u}", tag=f"bank{u}")
            for t in range(PACK):
                for s in range(MEMBERS):
                    nc.tensor.matmul(
                        sums[u][:, block(t, P)],
                        members[u][:, t, s::MEMBERS],
                        identity[:],
                        start=s == 0,
                        stop=s == MEMBERS - 1,
                        is_transpose=True,
                    )

        def gate_turned(u):
            turned = keep.tile([P, PACK * P], F32, name=f"turned{u}")
            nc.scalar.activation(turned[:], sums[u][:], ACT.Sigmoid)
            gates[u] = psum.tile([P, PACK, CHUNK], F32, name=f"gates{u}", tag=f"bank{TURNED + u}")
            for t in range(PACK):
                nc.tensor.transpose(gates[u][:, t, :], turned[:, block(t, P)], identity[:])

        def add_plain(u, places):
            view = members[u][:].rearrange("p t (j s e) -> p t j s e", s=2, e=2)
            for a in range(2):
                planes = block(a, 2)
                nc.vector.tensor_tensor(
                    pairs[u][:, planes, places, :], view[:, planes, places, 0, :], view[:, planes, places, 1, :], ALU.add
                )
            nc.vector.tensor_tensor(sums[u][:, :, places], pairs[u][:, :, places, 0], pairs[u][:, :, places, 1], ALU.add)

        def gate_plain(u, places):
            nc.scalar.activation(gates[u][:, :, places], sums[u][:, :, places], ACT.Sigmoid)

        def hidden(u, places):
            cols = slice(u * CHUNK + places.start, u * CHUNK + places.stop)
            grouped = z_bf[u][:, places.start * PACK : places.stop * PACK]
            nc.vector.tensor_tensor(
                grouped.rearrange("p (c i t) -> p c t i", i=4, t=PACK),
                gates[u][:, :, places].rearrange("p t (c i) -> p c t i", i=4),
                y_gain[:, :, cols].rearrange("p t (c i) -> p c t i", i=4),
                ALU.mult,
            )
            quantize(z_mx, cols, grouped)

        def second_layer(u):
            cols = block(u, CHUNK)
            for m in range(ROW_TILES):
                if u < CHUNKS - 1:
                    dst, stop = h_early[m][:, cols], u == CHUNKS - 2
                else:
                    dst, stop = h_last[m // 2][:, m % 2, :], m % 2 == 1
                product(dst, w2_mx, block(m, P), z_mx, cols, False, stop)

        def round_weight(raw, name):
            grouped = keep.tile([P, N * PACK], BF16, name=name, align_bytes=64)
            dst = grouped[:].rearrange("p (c j) -> p c j", j=PACK)
            nc.gpsimd.tensor_scalar(dst, raw[:].rearrange("p j c -> p c j"), 1.0, 0.0, ALU.mult, ALU.add)
            return grouped

        third, last = CHUNKS - 2, CHUNKS - 1
        whole = slice(0, CHUNK)
        halves = [block(a, CHUNK // 2) for a in range(2)]
        for u in (third, last):
            pairs[u] = keep.tile([P, PACK, CHUNK, 2], F32, name=f"pairs{u}", tag=f"pairs{u}", align_bytes=64)
            gates[u] = keep.tile([P, PACK, CHUNK], F32, name=f"gates{u}", tag=f"gates{u}", align_bytes=64)
        sums[third] = members[last][:, :, 2 * CHUNK : 3 * CHUNK]
        sums[last] = keep.tile([P, PACK, CHUNK], F32, name="sums_last", tag="sums_last", align_bytes=64)

        for t in range(PACK):
            nc.gpsimd.tensor_scalar(y_gain[:, t, :], y[t][:, :S], gain[:, t : t + 1], 0.0, ALU.mult, ALU.add)
        w3_bf = round_weight(w3_raw, "w3_bf")
        w2_bf = round_weight(w2_raw, "w2_bf")

        for u in range(TURNED):
            fetch_members(u, whole, VECTOR_PLANES_TURNED)
            add_turned(u)
        fetch_members(third, whole, VECTOR_PLANES_PLAIN)
        gate_turned(0)
        quantize(w3_mx, slice(0, N), w3_bf[:])
        quantize(w2_mx, slice(0, N), w2_bf[:])
        add_plain(third, whole)
        fetch_members(last, halves[0], VECTOR_PLANES_PLAIN)
        gate_turned(1)
        gate_plain(third, whole)

        h_last = [psum.tile([P, 2, CHUNK], F32, name=f"h_last{a}", tag=f"bank{a}") for a in range(2)]
        for m in range(ROW_TILES):
            rows = block(m, P)
            product(h_early[m][:, : 2 * CHUNK], w3_mx, rows, x_two, slice(0, 2 * CHUNK), True, False)
            product(h_early[m][:, 2 * CHUNK :], w3_mx, rows, x_two, block(third, CHUNK), False, False)
            product(h_last[m // 2][:, m % 2, :], w3_mx, rows, x_two, block(last, CHUNK), m % 2 == 0, False)

        hidden(0, whole)
        second_layer(0)
        add_plain(last, halves[0])
        gate_plain(last, halves[0])
        fetch_members(last, halves[1], 0)
        for u in (1, third):
            hidden(u, whole)
            second_layer(u)
        add_plain(last, halves[1])
        hidden(last, halves[0])
        gate_plain(last, halves[1])
        hidden(last, halves[1])
        second_layer(last)

        tiles = range(ROW_TILES)
        h_tags = ("h0", "sums_last", f"pairs{last}", f"gates{last}")
        h = [keep.tile([P, S], F32, name=f"h{m}", tag=h_tags[m], align_bytes=64) for m in tiles]
        st = [keep.tile([P, S], F32, name=f"st{m}") for m in tiles]
        su = [keep.tile([P, S], F32, name=f"su{m}") for m in tiles]
        picked = [keep.tile([P, S], F32, name=f"picked{m}") for m in tiles]
        result = [keep.tile([P, S], F32, name=f"result{m}") for m in tiles]

        def gather_shared(m, window, offsets, scalar_cols):
            cut = LANES * scalar_cols
            gather(False, picked[m][:, :cut], window[:], offsets[:, :scalar_cols])
            gather(True, picked[m][:, cut:], window[:], offsets[:, scalar_cols:])

        for m in tiles:
            nc.scalar.copy(out=h[m][:, :EARLY], in_=h_early[m][:])
        for m in tiles:
            copy = nc.vector.tensor_copy if m // 2 else nc.scalar.copy
            copy(out=h[m][:, EARLY:], in_=h_last[m // 2][:, m % 2, :])
        for m in tiles:
            gather_shared(m, h[m], n2_sb, SCALAR_COLS_FIRST)
            nc.vector.tensor_tensor(st[m][:], h[m][:], picked[m][:], ALU.subtract)
        for m in tiles:
            gather_shared(m, st[m], n3_sb, SCALAR_COLS)
            nc.vector.tensor_tensor(su[m][:], st[m][:], picked[m][:], ALU.max)
        for m in tiles:
            gather_shared(m, su[m], n4_sb, SCALAR_COLS)
            pieces = 2 if m == ROW_TILES - 1 else 1
            for a in range(pieces):
                cols = block(a, S // pieces)
                nc.vector.scalar_tensor_tensor(
                    result[m][:, cols], picked[m][:, cols], 0.5, su[m][:, cols], ALU.mult, ALU.add
                )
                nc.sync.dma_start(out=out[block(m, P), cols], in_=result[m][:, cols])
